import numpy as np
import ml_dtypes


def mxq(x, axis, fmt="e4m3"):
    dtype, down = {"e4m3": (ml_dtypes.float8_e4m3fn, 7), "e5m2": (ml_dtypes.float8_e5m2, 14)}[fmt]
    v = np.moveaxis(np.asarray(x, np.float32).astype(ml_dtypes.bfloat16).astype(np.float64), axis, -1)
    blocks = v.reshape(v.shape[:-1] + (-1, 32))
    amax = np.abs(blocks).max(-1, keepdims=True)
    byte = np.maximum(np.where(amax > 0, np.frexp(amax)[1] - 1 + 127, 0) - down, 1)
    scale = np.exp2(byte - 127.0)
    codes = (blocks / scale).astype(np.float32).astype(dtype).astype(np.float64)
    return np.moveaxis((codes * scale).reshape(v.shape), -1, axis)


WIDE = False


def mx_kscale(k):
    if not WIDE:
        return np.ones(k)
    levels = np.array([30, -30])
    if k % 512:
        return np.exp2(np.random.permutation(np.resize(levels, k // 32))).repeat(32)
    a = np.empty((k // 512, 16))
    for p in range(k // 512):
        a[p, :8] = np.random.permutation(np.resize(levels, 8))
        for g in range(8):
            far = levels[np.abs(levels - a[p, g]) >= 10]
            a[p, g + 8] = far[np.random.randint(len(far))]
    return np.exp2(a.ravel()).repeat(32)


def f64(x):
    return np.asarray(x).astype(np.float64)


E2M1 = np.array([0.0, 0.5, 1.0, 1.5, 2.0, 3.0, 4.0, 6.0, -0.0, -0.5, -1.0, -1.5, -2.0, -3.0, -4.0, -6.0])


def pack_weight(w, fmt):
    k, n = w.shape
    w = f64(np.asarray(w, np.float32).astype(ml_dtypes.bfloat16)).reshape(k // 32, 32, n)
    amax = np.abs(w).max(1)
    if fmt == "e4m3":
        byte = np.frexp(amax)[1] - 1 + 127 - 7
    else:
        mant, ex = np.frexp(amax / 6.0)
        byte = np.where(mant > 0.5, ex, ex - 1) + 127
    byte = np.clip(np.where(amax > 0, byte, 1), 1, 254)
    scaled = (w * np.exp2(127.0 - byte)[:, None, :]).reshape(k, n).astype(np.float32)
    by_word = np.ascontiguousarray(scaled.reshape(k // 512, 128, 4, n).transpose(0, 1, 3, 2))
    if fmt == "e4m3":
        words = by_word.astype(ml_dtypes.float8_e4m3fn).view(np.uint8)
    else:
        c = by_word.astype(ml_dtypes.float4_e2m1fn).view(np.uint8) & 0xF
        words = (c[..., 0::2] | (c[..., 1::2] << 4)).reshape(k // 512, 128, 2 * n)
    return np.ascontiguousarray(words), np.ascontiguousarray(byte.astype(np.uint8).reshape(k // 512, 16, n))


def unpack_weight(words, scales, fmt):
    g, _, n = scales.shape
    words = np.ascontiguousarray(words).reshape(g, 128, n, -1)
    if fmt == "e4m3":
        vals = words.view(ml_dtypes.float8_e4m3fn).astype(np.float64)
    else:
        nib = np.empty((g, 128, n, 4), np.uint8)
        nib[..., 0::2] = words & 0xF
        nib[..., 1::2] = words >> 4
        vals = E2M1[nib]
    vals = vals * np.repeat(np.exp2(scales.astype(np.float64) - 127.0), 8, axis=1)[..., None]
    return vals.transpose(0, 1, 3, 2).reshape(g * 512, n)


K, O, T, R, N = 1024, 512, 512, 512, 1536


def setup_inputs():
    n = np.random.standard_normal
    s = mx_kscale(K)[:, None]
    u = mx_kscale(T)[:, None]
    m = np.exp(0.5 * n((O + T, 1)))
    ux = mx_kscale(O)[:, None]
    p_hs = pack_weight(n((O, R)) * ux, "e4m3")
    return {
        "x": (n((K, T)) * s * u.T).astype(np.float32),
        "dn": (n((K, R)) / np.sqrt(K) / s).astype(np.float32),
        "hs_words": p_hs[0],
        "hs_scales": p_hs[1],
        "dy0": (m[:O] * n((O, N)) / np.sqrt(O + T) / ux).astype(np.float32),
        "dy1": (m[O:] * n((T, N)) / np.sqrt(O + T) / u).astype(np.float32),
    }


def reference(x, dn, hs_words, hs_scales, dy0, dy1):
    x_ = mxq(f64(x), 0, "e4m3")
    dn_ = mxq(f64(dn), 0, "e4m3")
    h = x_.T @ dn_
    h_ = mxq(h, 0, "e4m3")
    hs_ = unpack_weight(hs_words, hs_scales, "e4m3")
    dy0_ = mxq(f64(dy0), 0, "e5m2")
    dy1_ = mxq(f64(dy1), 0, "e5m2")
    db = hs_.T @ dy0_ + h_.T @ dy1_
    return db

@@ -1,0 +1,195 @@
+from contextlib import ExitStack
+
+import concourse.mybir as mybir
+
+K, O, T, R, N = 1024, 512, 512, 512, 1536
+FLOPS = 2 * K * T * R + 2 * (O + T) * R * N
+
+F32 = mybir.dt.float32
+BF16 = mybir.dt.bfloat16
+U32 = mybir.dt.uint32
+I32 = mybir.dt.int32
+U8 = mybir.dt.uint8
+E4M3 = mybir.dt.float8_e4m3fn_x4
+E5M2 = mybir.dt.float8_e5m2_x4
+
+P = 128
+PACK = 4
+W = 512
+HALF = W // 2
+QUARTER = W // 4
+CHUNKS = N // W
+BLOCKS = R // P
+
+
+def tile_mix_lorab_none_kernel(tc, x, dn, hs_words, hs_scales, dy0, dy1, out):
+    nc = tc.nc
+    with ExitStack() as ctx:
+        sb = ctx.enter_context(tc.tile_pool(name="sb", bufs=1))
+        ps = ctx.enter_context(tc.psum_pool(name="ps", bufs=1))
+        ctx.enter_context(tc.manual_schedule())
+
+        def load(name, rows):
+            raw = sb.tile([P, PACK, W], F32, name=name + "_raw")
+            nc.sync.dma_start(out=raw[:], in_=rows.rearrange("(p j) w -> p j w", j=PACK))
+            return raw
+
+        def operand(name, width):
+            codes = sb.tile([P, width], U32, name=name + "_codes", align_bytes=64)
+            scales = sb.tile([P, width], U8, name=name + "_scales", align_bytes=64)
+            return codes, scales
+
+        def interleave(copy, dst, src):
+            copy(
+                out=dst.rearrange("p (c i j) -> p c j i", i=4, j=PACK),
+                in_=src.rearrange("p j (c i) -> p c j i", i=4),
+            )
+
+        def quantize(op, c0, c1, src, fmt):
+            nc.vector.quantize_mx(out=op[0][:, c0:c1].bitcast(fmt), scales=op[1][:, c0:c1], in_=src)
+
+        staged = {}
+
+        def scalar_share(name, raw):
+            tail = sb.tile([P, HALF * PACK], BF16, name=name + "_tail", align_bytes=64)
+            staged[name] = tail
+            interleave(nc.scalar.copy, tail[:, QUARTER * PACK :], raw[:, :, HALF + QUARTER :])
+
+        def vector_share(name, raw, fmt):
+            tail = staged[name]
+            head = sb.tile([P, HALF * PACK], BF16, name=name + "_head", align_bytes=64)
+            op = operand(name, W)
+            interleave(nc.vector.tensor_copy, head[:], raw[:, :, :HALF])
+            interleave(nc.vector.tensor_copy, tail[:, : QUARTER * PACK], raw[:, :, HALF : HALF + QUARTER])
+            quantize(op, 0, HALF, head[:], fmt)
+            quantize(op, HALF, W, tail[:], fmt)
+            return op
+
+        def quantize_x(name, raw):
+            grouped = sb.tile([P, W * PACK], BF16, name=name + "_grouped", align_bytes=64)
+            op = operand(name, W)
+            nc.vector.tensor_copy(
+                out=grouped[:].rearrange("p (i m j) -> p m j i", i=PACK, j=PACK),
+                in_=raw[:].rearrange("p j (m i) -> p m j i", i=PACK),
+            )
+            quantize(op, 0, W, grouped[:], E4M3)
+            return op
+
+        def mx(acc, lhs, l0, lfmt, rhs, r0, rw, rfmt, start, stop):
+            nc.tensor.matmul_mx(
+                out=acc,
+                lhsT=lhs[0][:, l0 : l0 + P].bitcast(lfmt),
+                lhsT_scale=lhs[1][:, l0 : l0 + P],
+                rhs=rhs[0][:, r0 : r0 + rw].bitcast(rfmt),
+                rhs_scale=rhs[1][:, r0 : r0 + rw],
+                start=start,
+                stop=stop,
+            )
+
+        hs = operand("hs", R)
+        nc.vector.memset(hs[1][:].bitcast(I32), 0)
+        x_raw = [None, None]
+        dn_raw = [None, None]
+        x_raw[0] = load("x0", x[0:W, :])
+        for q in range(4):
+            nc.scalar.dma_start(
+                out=hs[1][32 * q : 32 * q + 4, :].bitcast(I32),
+                in_=hs_scales[0, 4 * q : 4 * q + 4, :].bitcast(I32),
+            )
+        dn_raw[0] = load("dn0", dn[0:W, :])
+        x_raw[1] = load("x1", x[W : 2 * W, :])
+        dn_raw[1] = load("dn1", dn[W : 2 * W, :])
+        nc.sync.dma_start(
+            out=hs[0][:].bitcast(I32), in_=hs_words[0].rearrange("p r i -> p (r i)").bitcast(I32)
+        )
+        dy0_raw = []
+        dy1_raw = []
+        for c in range(CHUNKS):
+            dy0_raw.append(load("dy0_%d" % c, dy0[:, c * W : (c + 1) * W]))
+            dy1_raw.append(load("dy1_%d" % c, dy1[:, c * W : (c + 1) * W]))
+
+        xq = []
+        dnq = []
+        for g in range(2):
+            xq.append(quantize_x("x%d" % g, x_raw[g]))
+            scalar_share("dn%d" % g, dn_raw[g])
+            dnq.append(vector_share("dn%d" % g, dn_raw[g], E4M3))
+
+        h_bank = []
+        for b in range(BLOCKS):
+            bank = ps.tile([P, PACK, P], F32, name="h_bank", tag="bank%d" % b)
+            h_bank.append(bank)
+            for i in range(PACK):
+                for g in range(2):
+                    mx(bank[:, i, :], xq[g], i * P, E4M3, dnq[g], b * P, P, E4M3, g == 0, g == 1)
+
+        h_bf = sb.tile([P, R * PACK], BF16, name="h_bf", align_bytes=64)
+        hq = operand("h", R)
+
+        def h_out(b):
+            nc.scalar.copy(
+                out=h_bf[:, b * W : (b + 1) * W].rearrange("p (n i) -> p n i", i=PACK),
+                in_=h_bank[b][:].rearrange("p i n -> p n i"),
+            )
+
+        def first_products(c, dyq):
+            banks = []
+            for b in range(BLOCKS):
+                bank = ps.tile([P, W], F32, name="o_bank", tag="bank%d" % (b + BLOCKS * ((c + 1) % 2)))
+                banks.append(bank)
+                mx(bank[:], hs, b * P, E4M3, dyq, 0, W, E5M2, True, False)
+            return banks
+
+        def second_products(banks, dyq):
+            for b in range(BLOCKS):
+                mx(banks[b][:], hq, b * P, E4M3, dyq, 0, W, E5M2, False, True)
+
+        res = [sb.tile([P, BLOCKS, W], F32, name="res%d" % c) for c in range(CHUNKS)]
+
+        def store(c, b0, b1):
+            nc.sync.dma_start(
+                out=out[b0 * P : b1 * P, c * W : (c + 1) * W].rearrange("(b p) n -> p b n", p=P),
+                in_=res[c][:, b0:b1, :],
+            )
+
+        scalar_share("dy0_0", dy0_raw[0])
+        q0 = vector_share("dy0_0", dy0_raw[0], E5M2)
+        banks0 = first_products(0, q0)
+        h_out(0)
+        h_out(1)
+        scalar_share("dy1_0", dy1_raw[0])
+        h_out(2)
+        h_out(3)
+        q1 = vector_share("dy1_0", dy1_raw[0], E5M2)
+        quantize(hq, 0, HALF, h_bf[:, : 2 * W], E4M3)
+        quantize(hq, HALF, R, h_bf[:, 2 * W :], E4M3)
+        second_products(banks0, q1)
+
+        scalar_share("dy0_1", dy0_raw[1])
+        q0 = vector_share("dy0_1", dy0_raw[1], E5M2)
+        banks1 = first_products(1, q0)
+        nc.scalar.copy(out=res[0][:, 0, :], in_=banks0[0][:])
+        nc.scalar.copy(out=res[0][:, 1, :], in_=banks0[1][:])
+        scalar_share("dy1_1", dy1_raw[1])
+        nc.scalar.copy(out=res[0][:, 2, :], in_=banks0[2][:])
+        nc.scalar.copy(out=res[0][:, 3, :], in_=banks0[3][:])
+        store(0, 0, BLOCKS)
+        q1 = vector_share("dy1_1", dy1_raw[1], E5M2)
+        second_products(banks1, q1)
+
+        scalar_share("dy0_2", dy0_raw[2])
+        q0 = vector_share("dy0_2", dy0_raw[2], E5M2)
+        banks2 = first_products(2, q0)
+        nc.scalar.copy(out=res[1][:, 0, :], in_=banks1[0][:])
+        nc.scalar.copy(out=res[1][:, 1, :], in_=banks1[1][:])
+        store(1, 0, 2)
+        nc.scalar.copy(out=res[1][:, 2, :], in_=banks1[2][:])
+        nc.vector.tensor_copy(out=res[1][:, 3, :], in_=banks1[3][:])
+        store(1, 2, 4)
+        scalar_share("dy1_2", dy1_raw[2])
+        q1 = vector_share("dy1_2", dy1_raw[2], E5M2)
+        second_products(banks2, q1)
+        for b in range(BLOCKS):
+            copy = nc.vector.tensor_copy if b % 2 == 0 else nc.scalar.copy
+            copy(out=res[2][:, b, :], in_=banks2[b][:])
+            store(2, b, b + 1)

@@ -18,7 +18,6 @@ PACK = 4
 W = 512
 HALF = W // 2
 QUARTER = W // 4
-CHUNKS = N // W
 BLOCKS = R // P
 
 
@@ -30,7 +29,7 @@ def tile_mix_lorab_none_kernel(tc, x, dn, hs_words, hs_scales, dy0, dy1, out):
         ctx.enter_context(tc.manual_schedule())
 
         def load(name, rows):
-            raw = sb.tile([P, PACK, W], F32, name=name + "_raw")
+            raw = sb.tile([P, PACK, rows.shape[1]], F32, name=name + "_raw")
             nc.sync.dma_start(out=raw[:], in_=rows.rearrange("(p j) w -> p j w", j=PACK))
             return raw
 
@@ -39,41 +38,19 @@ def tile_mix_lorab_none_kernel(tc, x, dn, hs_words, hs_scales, dy0, dy1, out):
             scales = sb.tile([P, width], U8, name=name + "_scales", align_bytes=64)
             return codes, scales
 
-        def interleave(copy, dst, src):
+        def staging(name, width):
+            return sb.tile([P, width * PACK], BF16, name=name + "_bf", align_bytes=64)
+
+        def cast(copy, bf, c0, c1, raw, first=0):
             copy(
-                out=dst.rearrange("p (c i j) -> p c j i", i=4, j=PACK),
-                in_=src.rearrange("p j (c i) -> p c j i", i=4),
+                out=bf[:, c0 * PACK : c1 * PACK].rearrange("p (c i j) -> p c j i", i=4, j=PACK),
+                in_=raw[:, :, c0 - first : c1 - first].rearrange("p j (c i) -> p c j i", i=4),
             )
 
-        def quantize(op, c0, c1, src, fmt):
-            nc.vector.quantize_mx(out=op[0][:, c0:c1].bitcast(fmt), scales=op[1][:, c0:c1], in_=src)
-
-        staged = {}
-
-        def scalar_share(name, raw):
-            tail = sb.tile([P, HALF * PACK], BF16, name=name + "_tail", align_bytes=64)
-            staged[name] = tail
-            interleave(nc.scalar.copy, tail[:, QUARTER * PACK :], raw[:, :, HALF + QUARTER :])
-
-        def vector_share(name, raw, fmt):
-            tail = staged[name]
-            head = sb.tile([P, HALF * PACK], BF16, name=name + "_head", align_bytes=64)
-            op = operand(name, W)
-            interleave(nc.vector.tensor_copy, head[:], raw[:, :, :HALF])
-            interleave(nc.vector.tensor_copy, tail[:, : QUARTER * PACK], raw[:, :, HALF : HALF + QUARTER])
-            quantize(op, 0, HALF, head[:], fmt)
-            quantize(op, HALF, W, tail[:], fmt)
-            return op
-
-        def quantize_x(name, raw):
-            grouped = sb.tile([P, W * PACK], BF16, name=name + "_grouped", align_bytes=64)
-            op = operand(name, W)
-            nc.vector.tensor_copy(
-                out=grouped[:].rearrange("p (i m j) -> p m j i", i=PACK, j=PACK),
-                in_=raw[:].rearrange("p j (m i) -> p m j i", i=PACK),
+        def quantize(op, c0, c1, bf, fmt):
+            nc.vector.quantize_mx(
+                out=op[0][:, c0:c1].bitcast(fmt), scales=op[1][:, c0:c1], in_=bf[:, c0 * PACK : c1 * PACK]
             )
-            quantize(op, 0, W, grouped[:], E4M3)
-            return op
 
         def mx(acc, lhs, l0, lfmt, rhs, r0, rw, rfmt, start, stop):
             nc.tensor.matmul_mx(
@@ -85,6 +62,9 @@ def tile_mix_lorab_none_kernel(tc, x, dn, hs_words, hs_scales, dy0, dy1, out):
                 start=start,
                 stop=stop,
             )
+
+        vcopy = nc.vector.tensor_copy
+        scopy = nc.scalar.copy
 
         hs = operand("hs", R)
         nc.vector.memset(hs[1][:].bitcast(I32), 0)
@@ -102,94 +82,117 @@ def tile_mix_lorab_none_kernel(tc, x, dn, hs_words, hs_scales, dy0, dy1, out):
         nc.sync.dma_start(
             out=hs[0][:].bitcast(I32), in_=hs_words[0].rearrange("p r i -> p (r i)").bitcast(I32)
         )
-        dy0_raw = []
-        dy1_raw = []
-        for c in range(CHUNKS):
-            dy0_raw.append(load("dy0_%d" % c, dy0[:, c * W : (c + 1) * W]))
-            dy1_raw.append(load("dy1_%d" % c, dy1[:, c * W : (c + 1) * W]))
+        a = []
+        b_ = []
+        for k in range(3):
+            a.append(load("a%d" % k, dy0[:, k * W : (k + 1) * W]))
+            b_.append(load("b%d" % k, dy1[:, k * W : (k + 1) * W]))
 
         xq = []
         dnq = []
         for g in range(2):
-            xq.append(quantize_x("x%d" % g, x_raw[g]))
-            scalar_share("dn%d" % g, dn_raw[g])
-            dnq.append(vector_share("dn%d" % g, dn_raw[g], E4M3))
+            grouped = staging("x%d" % g, W)
+            xq.append(operand("x%d" % g, W))
+            vcopy(
+                out=grouped[:].rearrange("p (i m j) -> p m j i", i=PACK, j=PACK),
+                in_=x_raw[g][:].rearrange("p j (m i) -> p m j i", i=PACK),
+            )
+            quantize(xq[g], 0, W, grouped, E4M3)
+            bf = staging("dn%d" % g, W)
+            dnq.append(operand("dn%d" % g, W))
+            cast(scopy, bf, W - QUARTER, W, dn_raw[g])
+            cast(vcopy, bf, 0, HALF, dn_raw[g])
+            cast(vcopy, bf, HALF, W - QUARTER, dn_raw[g])
+            quantize(dnq[g], 0, HALF, bf, E4M3)
+            quantize(dnq[g], HALF, W, bf, E4M3)
 
-        h_bank = []
-        for b in range(BLOCKS):
-            bank = ps.tile([P, PACK, P], F32, name="h_bank", tag="bank%d" % b)
-            h_bank.append(bank)
-            for i in range(PACK):
-                for g in range(2):
-                    mx(bank[:, i, :], xq[g], i * P, E4M3, dnq[g], b * P, P, E4M3, g == 0, g == 1)
+        h_bank = [ps.tile([P, PACK, P], F32, name="h_bank", tag="bank%d" % b) for b in range(BLOCKS)]
+        for g in range(2):
+            for b in range(BLOCKS):
+                for i in range(PACK):
+                    opens = g == 0 and i == 0
+                    closes = g == 1 and i == PACK - 1
+                    mx(h_bank[b][:, i, :], xq[g], i * P, E4M3, dnq[g], b * P, P, E4M3, opens, closes)
 
-        h_bf = sb.tile([P, R * PACK], BF16, name="h_bf", align_bytes=64)
+        h_bf = staging("h", R)
         hq = operand("h", R)
 
         def h_out(b):
-            nc.scalar.copy(
+            scopy(
                 out=h_bf[:, b * W : (b + 1) * W].rearrange("p (n i) -> p n i", i=PACK),
                 in_=h_bank[b][:].rearrange("p i n -> p n i"),
             )
 
-        def first_products(c, dyq):
-            banks = []
-            for b in range(BLOCKS):
-                bank = ps.tile([P, W], F32, name="o_bank", tag="bank%d" % (b + BLOCKS * ((c + 1) % 2)))
-                banks.append(bank)
-                mx(bank[:], hs, b * P, E4M3, dyq, 0, W, E5M2, True, False)
-            return banks
+        bf0 = staging("dy0", N)
+        bf1 = staging("dy1", N)
+        q0 = operand("dy0", N)
+        q1 = operand("dy1", N)
 
-        def second_products(banks, dyq):
-            for b in range(BLOCKS):
-                mx(banks[b][:], hq, b * P, E4M3, dyq, 0, W, E5M2, False, True)
+        banks = {}
+        res = sb.tile([P, BLOCKS, N], F32, name="res")
 
-        res = [sb.tile([P, BLOCKS, W], F32, name="res%d" % c) for c in range(CHUNKS)]
+        def opening(k, b):
+            banks[k, b] = ps.tile([P, W], F32, name="o_bank", tag="bank%d" % (b + BLOCKS * ((k + 1) % 2)))
+            mx(banks[k, b][:], hs, b * P, E4M3, q0, k * W, W, E5M2, True, False)
 
-        def store(c, b0, b1):
+        def closing(k, b):
+            mx(banks[k, b][:], hq, b * P, E4M3, q1, k * W, W, E5M2, False, True)
+
+        def drain(copy, k, b):
+            copy(out=res[:, b, k * W : (k + 1) * W], in_=banks[k, b][:])
+
+        def store(c0, c1, r0, r1):
             nc.sync.dma_start(
-                out=out[b0 * P : b1 * P, c * W : (c + 1) * W].rearrange("(b p) n -> p b n", p=P),
-                in_=res[c][:, b0:b1, :],
+                out=out[r0 * P : r1 * P, c0:c1].rearrange("(b p) n -> p b n", p=P),
+                in_=res[:, r0:r1, c0:c1],
             )
 
-        scalar_share("dy0_0", dy0_raw[0])
-        q0 = vector_share("dy0_0", dy0_raw[0], E5M2)
-        banks0 = first_products(0, q0)
+        def scalar_part(bf, raw, c0, first_col, share):
+            cast(scopy, bf, c0 + W - share, c0 + W, raw, first_col)
+
+        def wide(op, bf, raw, c0, first_col, share):
+            cast(vcopy, bf, c0, c0 + HALF, raw, first_col)
+            if share < HALF:
+                cast(vcopy, bf, c0 + HALF, c0 + W - share, raw, first_col)
+            quantize(op, c0, c0 + HALF, bf, E5M2)
+            quantize(op, c0 + HALF, c0 + W, bf, E5M2)
+
         h_out(0)
-        h_out(1)
-        scalar_share("dy1_0", dy1_raw[0])
-        h_out(2)
-        h_out(3)
-        q1 = vector_share("dy1_0", dy1_raw[0], E5M2)
-        quantize(hq, 0, HALF, h_bf[:, : 2 * W], E4M3)
-        quantize(hq, HALF, R, h_bf[:, 2 * W :], E4M3)
-        second_products(banks0, q1)
-
-        scalar_share("dy0_1", dy0_raw[1])
-        q0 = vector_share("dy0_1", dy0_raw[1], E5M2)
-        banks1 = first_products(1, q0)
-        nc.scalar.copy(out=res[0][:, 0, :], in_=banks0[0][:])
-        nc.scalar.copy(out=res[0][:, 1, :], in_=banks0[1][:])
-        scalar_share("dy1_1", dy1_raw[1])
-        nc.scalar.copy(out=res[0][:, 2, :], in_=banks0[2][:])
-        nc.scalar.copy(out=res[0][:, 3, :], in_=banks0[3][:])
-        store(0, 0, BLOCKS)
-        q1 = vector_share("dy1_1", dy1_raw[1], E5M2)
-        second_products(banks1, q1)
-
-        scalar_share("dy0_2", dy0_raw[2])
-        q0 = vector_share("dy0_2", dy0_raw[2], E5M2)
-        banks2 = first_products(2, q0)
-        nc.scalar.copy(out=res[1][:, 0, :], in_=banks1[0][:])
-        nc.scalar.copy(out=res[1][:, 1, :], in_=banks1[1][:])
-        store(1, 0, 2)
-        nc.scalar.copy(out=res[1][:, 2, :], in_=banks1[2][:])
-        nc.vector.tensor_copy(out=res[1][:, 3, :], in_=banks1[3][:])
-        store(1, 2, 4)
-        scalar_share("dy1_2", dy1_raw[2])
-        q1 = vector_share("dy1_2", dy1_raw[2], E5M2)
-        second_products(banks2, q1)
+        scalar_part(bf0, a[0], 0, 0, QUARTER)
+        for b in range(1, BLOCKS):
+            h_out(b)
+        wide(q0, bf0, a[0], 0, 0, QUARTER)
+        quantize(hq, 0, HALF, h_bf, E4M3)
         for b in range(BLOCKS):
-            copy = nc.vector.tensor_copy if b % 2 == 0 else nc.scalar.copy
-            copy(out=res[2][:, b, :], in_=banks2[b][:])
-            store(2, b, b + 1)
+            opening(0, b)
+        scalar_part(bf1, b_[0], 0, 0, QUARTER)
+        cast(vcopy, bf1, 0, HALF, b_[0], 0)
+        cast(vcopy, bf1, HALF, W - QUARTER, b_[0], 0)
+        quantize(q1, 0, HALF, bf1, E5M2)
+        quantize(q1, HALF, W, bf1, E5M2)
+        quantize(hq, HALF, R, h_bf, E4M3)
+        for b in range(BLOCKS):
+            closing(0, b)
+        wide(q0, bf0, a[1], W, W, 0)
+        for b in range(BLOCKS):
+            opening(1, b)
+        for b in range(4):
+            drain(scopy, 0, b)
+        scalar_part(bf1, b_[1], W, W, QUARTER)
+        store(0, W, 0, BLOCKS)
+        wide(q1, bf1, b_[1], W, W, QUARTER)
+        for b in range(BLOCKS):
+            closing(1, b)
+        wide(q0, bf0, a[2], 2 * W, 2 * W, 0)
+        for b in range(4):
+            opening(2, b)
+        for b in range(4):
+            drain(scopy, 1, b)
+        store(W, 2 * W, 0, BLOCKS)
+        scalar_part(bf1, b_[2], 2 * W, 2 * W, QUARTER)
+        wide(q1, bf1, b_[2], 2 * W, 2 * W, QUARTER)
+        for b in range(BLOCKS):
+            closing(2, b)
+        for b in range(BLOCKS):
+            drain(vcopy if b % 2 == 0 else scopy, 2, b)
+            store(2 * W, N, b, b + 1)

@@ -68,36 +68,41 @@ def tile_mix_lorab_none_kernel(tc, x, dn, hs_words, hs_scales, dy0, dy1, out):
 
         hs = operand("hs", R)
         nc.vector.memset(hs[1][:].bitcast(I32), 0)
-        x_raw = [None, None]
-        dn_raw = [None, None]
-        x_raw[0] = load("x0", x[0:W, :])
+
+        def load_passes(name, src):
+            raw = sb.tile([P, 2, PACK, W], F32, name=name + "_raw")
+            nc.sync.dma_start(out=raw[:], in_=src.rearrange("(g p j) w -> p g j w", g=2, j=PACK))
+            return [raw[:, 0], raw[:, 1]]
+
+        x_raw = load_passes("x", x)
         for q in range(4):
             nc.scalar.dma_start(
                 out=hs[1][32 * q : 32 * q + 4, :].bitcast(I32),
                 in_=hs_scales[0, 4 * q : 4 * q + 4, :].bitcast(I32),
             )
-        dn_raw[0] = load("dn0", dn[0:W, :])
-        x_raw[1] = load("x1", x[W : 2 * W, :])
-        dn_raw[1] = load("dn1", dn[W : 2 * W, :])
+        dn_raw = [load("dn0", dn[0:W, :]), load("dn1", dn[W:, :])]
+        a01 = load("a01", dy0[:, 0 : 2 * W])
         nc.sync.dma_start(
             out=hs[0][:].bitcast(I32), in_=hs_words[0].rearrange("p r i -> p (r i)").bitcast(I32)
         )
-        a = []
-        b_ = []
-        for k in range(3):
-            a.append(load("a%d" % k, dy0[:, k * W : (k + 1) * W]))
-            b_.append(load("b%d" % k, dy1[:, k * W : (k + 1) * W]))
+        b0 = load("b0", dy1[:, 0:W])
+        b1 = load("b1", dy1[:, W : 2 * W])
+        a2 = load("a2", dy0[:, 2 * W :])
+        b2 = load("b2", dy1[:, 2 * W :])
 
         xq = []
         dnq = []
-        for g in range(2):
+
+        def quantize_x(g):
             grouped = staging("x%d" % g, W)
             xq.append(operand("x%d" % g, W))
-            vcopy(
-                out=grouped[:].rearrange("p (i m j) -> p m j i", i=PACK, j=PACK),
-                in_=x_raw[g][:].rearrange("p j (m i) -> p m j i", i=PACK),
-            )
+            x_out = grouped[:].rearrange("p (i m j) -> p m j i", i=PACK, j=PACK)
+            x_in = x_raw[g][:].rearrange("p j (m i) -> p m j i", i=PACK)
+            scopy(out=x_out[:, 96:], in_=x_in[:, 96:])
+            vcopy(out=x_out[:, :96], in_=x_in[:, :96])
             quantize(xq[g], 0, W, grouped, E4M3)
+
+        def quantize_dn(g):
             bf = staging("dn%d" % g, W)
             dnq.append(operand("dn%d" % g, W))
             cast(scopy, bf, W - QUARTER, W, dn_raw[g])
@@ -105,6 +110,11 @@ def tile_mix_lorab_none_kernel(tc, x, dn, hs_words, hs_scales, dy0, dy1, out):
             cast(vcopy, bf, HALF, W - QUARTER, dn_raw[g])
             quantize(dnq[g], 0, HALF, bf, E4M3)
             quantize(dnq[g], HALF, W, bf, E4M3)
+
+        for g in range(2):
+            quantize_x(g)
+        for g in range(2):
+            quantize_dn(g)
 
         h_bank = [ps.tile([P, PACK, P], F32, name="h_bank", tag="bank%d" % b) for b in range(BLOCKS)]
         for g in range(2):
@@ -158,41 +168,38 @@ def tile_mix_lorab_none_kernel(tc, x, dn, hs_words, hs_scales, dy0, dy1, out):
             quantize(op, c0 + HALF, c0 + W, bf, E5M2)
 
         h_out(0)
-        scalar_part(bf0, a[0], 0, 0, QUARTER)
-        for b in range(1, BLOCKS):
-            h_out(b)
-        wide(q0, bf0, a[0], 0, 0, QUARTER)
-        quantize(hq, 0, HALF, h_bf, E4M3)
-        for b in range(BLOCKS):
-            opening(0, b)
-        scalar_part(bf1, b_[0], 0, 0, QUARTER)
-        cast(vcopy, bf1, 0, HALF, b_[0], 0)
-        cast(vcopy, bf1, HALF, W - QUARTER, b_[0], 0)
-        quantize(q1, 0, HALF, bf1, E5M2)
-        quantize(q1, HALF, W, bf1, E5M2)
-        quantize(hq, HALF, R, h_bf, E4M3)
+        h_out(1)
+        scalar_part(bf0, a01, 0, 0, QUARTER)
+        h_out(2)
+        h_out(3)
+        scalar_part(bf0, a01, W, 0, QUARTER)
+        for k in range(2):
+            wide(q0, bf0, a01, k * W, 0, QUARTER)
+            for b in range(BLOCKS):
+                opening(k, b)
+        scalar_part(bf1, b0, 0, 0, QUARTER)
+        quantize(hq, 0, R, h_bf, E4M3)
+        wide(q1, bf1, b0, 0, 0, QUARTER)
         for b in range(BLOCKS):
             closing(0, b)
-        wide(q0, bf0, a[1], W, W, 0)
-        for b in range(BLOCKS):
-            opening(1, b)
-        for b in range(4):
-            drain(scopy, 0, b)
-        scalar_part(bf1, b_[1], W, W, QUARTER)
-        store(0, W, 0, BLOCKS)
-        wide(q1, bf1, b_[1], W, W, QUARTER)
+        scalar_part(bf1, b1, W, W, QUARTER)
+        wide(q1, bf1, b1, W, W, QUARTER)
         for b in range(BLOCKS):
             closing(1, b)
-        wide(q0, bf0, a[2], 2 * W, 2 * W, 0)
-        for b in range(4):
+        for b in range(BLOCKS):
+            drain(vcopy if b == 1 else scopy, 0, b)
+        store(0, W, 0, BLOCKS)
+        wide(q0, bf0, a2, 2 * W, 2 * W, 0)
+        for b in range(BLOCKS):
             opening(2, b)
         for b in range(4):
             drain(scopy, 1, b)
         store(W, 2 * W, 0, BLOCKS)
-        scalar_part(bf1, b_[2], 2 * W, 2 * W, QUARTER)
-        wide(q1, bf1, b_[2], 2 * W, 2 * W, QUARTER)
+        scalar_part(bf1, b2, 2 * W, 2 * W, QUARTER)
+        wide(q1, bf1, b2, 2 * W, 2 * W, QUARTER)
         for b in range(BLOCKS):
             closing(2, b)
         for b in range(BLOCKS):
             drain(vcopy if b % 2 == 0 else scopy, 2, b)
-            store(2 * W, N, b, b + 1)
+            if b != 2:
+                store(2 * W, N, b if b < 2 else 2, b + 1)

@@ -19,6 +19,7 @@ W = 512
 HALF = W // 2
 QUARTER = W // 4
 BLOCKS = R // P
+SHARE = 192
 
 
 def tile_mix_lorab_none_kernel(tc, x, dn, hs_words, hs_scales, dy0, dy1, out):
@@ -69,19 +70,17 @@ def tile_mix_lorab_none_kernel(tc, x, dn, hs_words, hs_scales, dy0, dy1, out):
         hs = operand("hs", R)
         nc.vector.memset(hs[1][:].bitcast(I32), 0)
 
-        def load_passes(name, src):
-            raw = sb.tile([P, 2, PACK, W], F32, name=name + "_raw")
-            nc.sync.dma_start(out=raw[:], in_=src.rearrange("(g p j) w -> p g j w", g=2, j=PACK))
-            return [raw[:, 0], raw[:, 1]]
-
-        x_raw = load_passes("x", x)
+        a01 = load("a01", dy0[:, 0 : 2 * W])
         for q in range(4):
             nc.scalar.dma_start(
                 out=hs[1][32 * q : 32 * q + 4, :].bitcast(I32),
                 in_=hs_scales[0, 4 * q : 4 * q + 4, :].bitcast(I32),
             )
-        dn_raw = [load("dn0", dn[0:W, :]), load("dn1", dn[W:, :])]
-        a01 = load("a01", dy0[:, 0 : 2 * W])
+        x_raw = []
+        dn_raw = []
+        for g in range(2):
+            x_raw.append(load("x%d" % g, x[g * W : (g + 1) * W, :]))
+            dn_raw.append(load("dn%d" % g, dn[g * W : (g + 1) * W, :]))
         nc.sync.dma_start(
             out=hs[0][:].bitcast(I32), in_=hs_words[0].rearrange("p r i -> p (r i)").bitcast(I32)
         )
@@ -89,6 +88,22 @@ def tile_mix_lorab_none_kernel(tc, x, dn, hs_words, hs_scales, dy0, dy1, out):
         b1 = load("b1", dy1[:, W : 2 * W])
         a2 = load("a2", dy0[:, 2 * W :])
         b2 = load("b2", dy1[:, 2 * W :])
+
+        bf0 = staging("dy0", N)
+        bf1 = staging("dy1", N)
+        q0 = operand("dy0", N)
+        q1 = operand("dy1", N)
+
+        def piece(op, bf, raw, c0, first_col, share, fmt):
+            if share > 0:
+                cast(scopy, bf, c0 + W - share, c0 + W, raw, first_col)
+            vector_piece(op, bf, raw, c0, first_col, share, fmt)
+
+        def vector_piece(op, bf, raw, c0, first_col, share, fmt):
+            cast(vcopy, bf, c0, c0 + HALF, raw, first_col)
+            cast(vcopy, bf, c0 + HALF, c0 + W - share, raw, first_col)
+            quantize(op, c0, c0 + HALF, bf, fmt)
+            quantize(op, c0 + HALF, c0 + W, bf, fmt)
 
         xq = []
         dnq = []
@@ -98,45 +113,30 @@ def tile_mix_lorab_none_kernel(tc, x, dn, hs_words, hs_scales, dy0, dy1, out):
             xq.append(operand("x%d" % g, W))
             x_out = grouped[:].rearrange("p (i m j) -> p m j i", i=PACK, j=PACK)
             x_in = x_raw[g][:].rearrange("p j (m i) -> p m j i", i=PACK)
-            scopy(out=x_out[:, 96:], in_=x_in[:, 96:])
-            vcopy(out=x_out[:, :96], in_=x_in[:, :96])
+            scopy(out=x_out[:, 80:], in_=x_in[:, 80:])
+            vcopy(out=x_out[:, :80], in_=x_in[:, :80])
             quantize(xq[g], 0, W, grouped, E4M3)
 
         def quantize_dn(g):
-            bf = staging("dn%d" % g, W)
             dnq.append(operand("dn%d" % g, W))
-            cast(scopy, bf, W - QUARTER, W, dn_raw[g])
-            cast(vcopy, bf, 0, HALF, dn_raw[g])
-            cast(vcopy, bf, HALF, W - QUARTER, dn_raw[g])
-            quantize(dnq[g], 0, HALF, bf, E4M3)
-            quantize(dnq[g], HALF, W, bf, E4M3)
-
-        for g in range(2):
-            quantize_x(g)
-        for g in range(2):
-            quantize_dn(g)
+            piece(dnq[g], staging("dn%d" % g, W), dn_raw[g], 0, 0, SHARE, E4M3)
 
         h_bank = [ps.tile([P, PACK, P], F32, name="h_bank", tag="bank%d" % b) for b in range(BLOCKS)]
-        for g in range(2):
-            for b in range(BLOCKS):
-                for i in range(PACK):
-                    opens = g == 0 and i == 0
-                    closes = g == 1 and i == PACK - 1
-                    mx(h_bank[b][:, i, :], xq[g], i * P, E4M3, dnq[g], b * P, P, E4M3, opens, closes)
+
+        def h_pass(g, b):
+            for i in range(PACK):
+                opens = g == 0 and i == 0
+                closes = g == 1 and i == PACK - 1
+                mx(h_bank[b][:, i, :], xq[g], i * P, E4M3, dnq[g], b * P, P, E4M3, opens, closes)
 
         h_bf = staging("h", R)
         hq = operand("h", R)
 
-        def h_out(b):
-            scopy(
+        def h_out(copy, b):
+            copy(
                 out=h_bf[:, b * W : (b + 1) * W].rearrange("p (n i) -> p n i", i=PACK),
                 in_=h_bank[b][:].rearrange("p i n -> p n i"),
             )
-
-        bf0 = staging("dy0", N)
-        bf1 = staging("dy1", N)
-        q0 = operand("dy0", N)
-        q1 = operand("dy1", N)
 
         banks = {}
         res = sb.tile([P, BLOCKS, N], F32, name="res")
@@ -157,49 +157,52 @@ def tile_mix_lorab_none_kernel(tc, x, dn, hs_words, hs_scales, dy0, dy1, out):
                 in_=res[:, r0:r1, c0:c1],
             )
 
-        def scalar_part(bf, raw, c0, first_col, share):
-            cast(scopy, bf, c0 + W - share, c0 + W, raw, first_col)
-
-        def wide(op, bf, raw, c0, first_col, share):
-            cast(vcopy, bf, c0, c0 + HALF, raw, first_col)
-            if share < HALF:
-                cast(vcopy, bf, c0 + HALF, c0 + W - share, raw, first_col)
-            quantize(op, c0, c0 + HALF, bf, E5M2)
-            quantize(op, c0 + HALF, c0 + W, bf, E5M2)
-
-        h_out(0)
-        h_out(1)
-        scalar_part(bf0, a01, 0, 0, QUARTER)
-        h_out(2)
-        h_out(3)
-        scalar_part(bf0, a01, W, 0, QUARTER)
         for k in range(2):
-            wide(q0, bf0, a01, k * W, 0, QUARTER)
-            for b in range(BLOCKS):
-                opening(k, b)
-        scalar_part(bf1, b0, 0, 0, QUARTER)
-        quantize(hq, 0, R, h_bf, E4M3)
-        wide(q1, bf1, b0, 0, 0, QUARTER)
+            piece(q0, bf0, a01, k * W, 0, SHARE, E5M2)
+        quantize_x(0)
+        quantize_dn(0)
+        for b in range(BLOCKS):
+            h_pass(0, b)
+        quantize_x(1)
+        quantize_dn(1)
+        opening(0, 0)
+        opening(0, 1)
+        for b in range(BLOCKS):
+            h_pass(1, b)
+            h_out(vcopy if b == 1 else scopy, b)
+        opening(0, 2)
+        opening(0, 3)
+        for b in range(BLOCKS):
+            opening(1, b)
+
+        cast(vcopy, bf1, 0, HALF, b0)
+        cast(vcopy, bf1, HALF, W, b0)
+        quantize(hq, 0, HALF, h_bf, E4M3)
+        quantize(q1, 0, HALF, bf1, E5M2)
+        quantize(q1, HALF, W, bf1, E5M2)
+        quantize(hq, HALF, R, h_bf, E4M3)
         for b in range(BLOCKS):
             closing(0, b)
-        scalar_part(bf1, b1, W, W, QUARTER)
-        wide(q1, bf1, b1, W, W, QUARTER)
-        for b in range(BLOCKS):
+        vector_piece(q1, bf1, b1, W, W, 0, E5M2)
+        for b in (2, 3, 0, 1):
             closing(1, b)
-        for b in range(BLOCKS):
-            drain(vcopy if b == 1 else scopy, 0, b)
-        store(0, W, 0, BLOCKS)
-        wide(q0, bf0, a2, 2 * W, 2 * W, 0)
+        drain(scopy, 0, 0)
+        drain(scopy, 0, 1)
+        store(0, W, 0, 2)
+        drain(scopy, 0, 2)
+        drain(scopy, 0, 3)
+        for b in (2, 3):
+            drain(scopy, 1, b)
+            store(0, 2 * W, b, b + 1)
+        vector_piece(q0, bf0, a2, 2 * W, 2 * W, 0, E5M2)
         for b in range(BLOCKS):
             opening(2, b)
-        for b in range(4):
-            drain(scopy, 1, b)
-        store(W, 2 * W, 0, BLOCKS)
-        scalar_part(bf1, b2, 2 * W, 2 * W, QUARTER)
-        wide(q1, bf1, b2, 2 * W, 2 * W, QUARTER)
+        drain(scopy, 1, 0)
+        piece(q1, bf1, b2, 2 * W, 2 * W, SHARE, E5M2)
+        drain(scopy, 1, 1)
+        store(W, 2 * W, 0, 2)
         for b in range(BLOCKS):
             closing(2, b)
         for b in range(BLOCKS):
             drain(vcopy if b % 2 == 0 else scopy, 2, b)
-            if b != 2:
-                store(2 * W, N, b if b < 2 else 2, b + 1)
+            store(2 * W, N, b, b + 1)

@@ -17,9 +17,11 @@ P = 128
 PACK = 4
 W = 512
 HALF = W // 2
-QUARTER = W // 4
+RUN = 4
 BLOCKS = R // P
+PASSES = K // W
 SHARE = 192
+LAST_SHARE = 160
 
 
 def tile_mix_lorab_none_kernel(tc, x, dn, hs_words, hs_scales, dy0, dy1, out):
@@ -28,6 +30,9 @@ def tile_mix_lorab_none_kernel(tc, x, dn, hs_words, hs_scales, dy0, dy1, out):
         sb = ctx.enter_context(tc.tile_pool(name="sb", bufs=1))
         ps = ctx.enter_context(tc.psum_pool(name="ps", bufs=1))
         ctx.enter_context(tc.manual_schedule())
+
+        vcopy = nc.vector.tensor_copy
+        scopy = nc.scalar.copy
 
         def load(name, rows):
             raw = sb.tile([P, PACK, rows.shape[1]], F32, name=name + "_raw")
@@ -44,14 +49,22 @@ def tile_mix_lorab_none_kernel(tc, x, dn, hs_words, hs_scales, dy0, dy1, out):
 
         def cast(copy, bf, c0, c1, raw, first=0):
             copy(
-                out=bf[:, c0 * PACK : c1 * PACK].rearrange("p (c i j) -> p c j i", i=4, j=PACK),
-                in_=raw[:, :, c0 - first : c1 - first].rearrange("p j (c i) -> p c j i", i=4),
+                out=bf[:, c0 * PACK : c1 * PACK].rearrange("p (c i j) -> p c j i", i=RUN, j=PACK),
+                in_=raw[:, :, c0 - first : c1 - first].rearrange("p j (c i) -> p c j i", i=RUN),
             )
 
         def quantize(op, c0, c1, bf, fmt):
             nc.vector.quantize_mx(
                 out=op[0][:, c0:c1].bitcast(fmt), scales=op[1][:, c0:c1], in_=bf[:, c0 * PACK : c1 * PACK]
             )
+
+        def piece(op, bf, raw, c0, first, share, fmt):
+            if share > 0:
+                cast(scopy, bf, c0 + W - share, c0 + W, raw, first)
+            cast(vcopy, bf, c0, c0 + HALF, raw, first)
+            cast(vcopy, bf, c0 + HALF, c0 + W - share, raw, first)
+            quantize(op, c0, c0 + HALF, bf, fmt)
+            quantize(op, c0 + HALF, c0 + W, bf, fmt)
 
         def mx(acc, lhs, l0, lfmt, rhs, r0, rw, rfmt, start, stop):
             nc.tensor.matmul_mx(
@@ -64,13 +77,9 @@ def tile_mix_lorab_none_kernel(tc, x, dn, hs_words, hs_scales, dy0, dy1, out):
                 stop=stop,
             )
 
-        vcopy = nc.vector.tensor_copy
-        scopy = nc.scalar.copy
-
         hs = operand("hs", R)
         nc.vector.memset(hs[1][:].bitcast(I32), 0)
-
-        a01 = load("a01", dy0[:, 0 : 2 * W])
+        dy0_head = load("dy0_head", dy0[:, 0 : 2 * W])
         for q in range(4):
             nc.scalar.dma_start(
                 out=hs[1][32 * q : 32 * q + 4, :].bitcast(I32),
@@ -78,64 +87,48 @@ def tile_mix_lorab_none_kernel(tc, x, dn, hs_words, hs_scales, dy0, dy1, out):
             )
         x_raw = []
         dn_raw = []
-        for g in range(2):
+        for g in range(PASSES):
             x_raw.append(load("x%d" % g, x[g * W : (g + 1) * W, :]))
             dn_raw.append(load("dn%d" % g, dn[g * W : (g + 1) * W, :]))
         nc.sync.dma_start(
             out=hs[0][:].bitcast(I32), in_=hs_words[0].rearrange("p r i -> p (r i)").bitcast(I32)
         )
-        b0 = load("b0", dy1[:, 0:W])
-        b1 = load("b1", dy1[:, W : 2 * W])
-        a2 = load("a2", dy0[:, 2 * W :])
-        b2 = load("b2", dy1[:, 2 * W :])
+        dy1_raw = [load("dy1_%d" % k, dy1[:, k * W : (k + 1) * W]) for k in range(2)]
+        dy0_last = load("dy0_last", dy0[:, 2 * W :])
+        dy1_last = load("dy1_last", dy1[:, 2 * W :])
 
-        bf0 = staging("dy0", N)
-        bf1 = staging("dy1", N)
-        q0 = operand("dy0", N)
-        q1 = operand("dy1", N)
-
-        def piece(op, bf, raw, c0, first_col, share, fmt):
-            if share > 0:
-                cast(scopy, bf, c0 + W - share, c0 + W, raw, first_col)
-            vector_piece(op, bf, raw, c0, first_col, share, fmt)
-
-        def vector_piece(op, bf, raw, c0, first_col, share, fmt):
-            cast(vcopy, bf, c0, c0 + HALF, raw, first_col)
-            cast(vcopy, bf, c0 + HALF, c0 + W - share, raw, first_col)
-            quantize(op, c0, c0 + HALF, bf, fmt)
-            quantize(op, c0 + HALF, c0 + W, bf, fmt)
-
-        xq = []
-        dnq = []
+        dy0_bf = staging("dy0", N)
+        dy1_bf = staging("dy1", N)
+        dy0_q = operand("dy0", N)
+        dy1_q = operand("dy1", N)
+        x_bf = [staging("x%d" % g, T) for g in range(PASSES)]
+        x_q = [operand("x%d" % g, T) for g in range(PASSES)]
+        dn_bf = [staging("dn%d" % g, R) for g in range(PASSES)]
+        dn_q = [operand("dn%d" % g, R) for g in range(PASSES)]
 
         def quantize_x(g):
-            grouped = staging("x%d" % g, W)
-            xq.append(operand("x%d" % g, W))
-            x_out = grouped[:].rearrange("p (i m j) -> p m j i", i=PACK, j=PACK)
+            x_out = x_bf[g][:].rearrange("p (i m j) -> p m j i", i=PACK, j=PACK)
             x_in = x_raw[g][:].rearrange("p j (m i) -> p m j i", i=PACK)
-            scopy(out=x_out[:, 80:], in_=x_in[:, 80:])
-            vcopy(out=x_out[:, :80], in_=x_in[:, :80])
-            quantize(xq[g], 0, W, grouped, E4M3)
-
-        def quantize_dn(g):
-            dnq.append(operand("dn%d" % g, W))
-            piece(dnq[g], staging("dn%d" % g, W), dn_raw[g], 0, 0, SHARE, E4M3)
+            cut = (T - SHARE) // PACK
+            scopy(out=x_out[:, cut:], in_=x_in[:, cut:])
+            vcopy(out=x_out[:, :cut], in_=x_in[:, :cut])
+            quantize(x_q[g], 0, T, x_bf[g], E4M3)
 
         h_bank = [ps.tile([P, PACK, P], F32, name="h_bank", tag="bank%d" % b) for b in range(BLOCKS)]
 
         def h_pass(g, b):
             for i in range(PACK):
                 opens = g == 0 and i == 0
-                closes = g == 1 and i == PACK - 1
-                mx(h_bank[b][:, i, :], xq[g], i * P, E4M3, dnq[g], b * P, P, E4M3, opens, closes)
+                closes = g == PASSES - 1 and i == PACK - 1
+                mx(h_bank[b][:, i, :], x_q[g], i * P, E4M3, dn_q[g], b * P, P, E4M3, opens, closes)
 
         h_bf = staging("h", R)
-        hq = operand("h", R)
+        h_q = operand("h", R)
 
         def h_out(copy, b):
             copy(
-                out=h_bf[:, b * W : (b + 1) * W].rearrange("p (n i) -> p n i", i=PACK),
-                in_=h_bank[b][:].rearrange("p i n -> p n i"),
+                out=h_bf[:, b * W : (b + 1) * W].rearrange("p (r i) -> p r i", i=PACK),
+                in_=h_bank[b][:].rearrange("p i r -> p r i"),
             )
 
         banks = {}
@@ -143,47 +136,55 @@ def tile_mix_lorab_none_kernel(tc, x, dn, hs_words, hs_scales, dy0, dy1, out):
 
         def opening(k, b):
             banks[k, b] = ps.tile([P, W], F32, name="o_bank", tag="bank%d" % (b + BLOCKS * ((k + 1) % 2)))
-            mx(banks[k, b][:], hs, b * P, E4M3, q0, k * W, W, E5M2, True, False)
+            mx(banks[k, b][:], hs, b * P, E4M3, dy0_q, k * W, W, E5M2, True, False)
 
         def closing(k, b):
-            mx(banks[k, b][:], hq, b * P, E4M3, q1, k * W, W, E5M2, False, True)
+            mx(banks[k, b][:], h_q, b * P, E4M3, dy1_q, k * W, W, E5M2, False, True)
 
         def drain(copy, k, b):
             copy(out=res[:, b, k * W : (k + 1) * W], in_=banks[k, b][:])
 
-        def store(c0, c1, r0, r1):
+        def store(c0, c1, b0, b1):
             nc.sync.dma_start(
-                out=out[r0 * P : r1 * P, c0:c1].rearrange("(b p) n -> p b n", p=P),
-                in_=res[:, r0:r1, c0:c1],
+                out=out[b0 * P : b1 * P, c0:c1].rearrange("(b p) n -> p b n", p=P),
+                in_=res[:, b0:b1, c0:c1],
             )
 
         for k in range(2):
-            piece(q0, bf0, a01, k * W, 0, SHARE, E5M2)
+            piece(dy0_q, dy0_bf, dy0_head, k * W, 0, SHARE, E5M2)
         quantize_x(0)
-        quantize_dn(0)
+        piece(dn_q[0], dn_bf[0], dn_raw[0], 0, 0, SHARE, E4M3)
         for b in range(BLOCKS):
             h_pass(0, b)
         quantize_x(1)
-        quantize_dn(1)
+
+        cast(scopy, dn_bf[1], 3 * P, 4 * P, dn_raw[1])
+        cast(vcopy, dn_bf[1], 0, P, dn_raw[1])
+        cast(vcopy, dn_bf[1], P, 2 * P, dn_raw[1])
+        quantize(dn_q[1], 0, P, dn_bf[1], E4M3)
+        cast(vcopy, dn_bf[1], 2 * P, 3 * P, dn_raw[1])
+        for b in (1, 3, 2):
+            quantize(dn_q[1], b * P, (b + 1) * P, dn_bf[1], E4M3)
+
         opening(0, 0)
-        opening(0, 1)
         for b in range(BLOCKS):
             h_pass(1, b)
             h_out(vcopy if b == 1 else scopy, b)
-        opening(0, 2)
-        opening(0, 3)
+        for b in range(1, BLOCKS):
+            opening(0, b)
         for b in range(BLOCKS):
             opening(1, b)
 
-        cast(vcopy, bf1, 0, HALF, b0)
-        cast(vcopy, bf1, HALF, W, b0)
-        quantize(hq, 0, HALF, h_bf, E4M3)
-        quantize(q1, 0, HALF, bf1, E5M2)
-        quantize(q1, HALF, W, bf1, E5M2)
-        quantize(hq, HALF, R, h_bf, E4M3)
+        cast(vcopy, dy1_bf, 0, HALF, dy1_raw[0])
+        cast(vcopy, dy1_bf, HALF, W, dy1_raw[0])
+        quantize(h_q, 0, HALF, h_bf, E4M3)
+        quantize(dy1_q, 0, HALF, dy1_bf, E5M2)
+        quantize(dy1_q, HALF, W, dy1_bf, E5M2)
+        quantize(h_q, HALF, R, h_bf, E4M3)
         for b in range(BLOCKS):
             closing(0, b)
-        vector_piece(q1, bf1, b1, W, W, 0, E5M2)
+        piece(dy1_q, dy1_bf, dy1_raw[1], W, W, 0, E5M2)
+
         for b in (2, 3, 0, 1):
             closing(1, b)
         drain(scopy, 0, 0)
@@ -194,13 +195,15 @@ def tile_mix_lorab_none_kernel(tc, x, dn, hs_words, hs_scales, dy0, dy1, out):
         for b in (2, 3):
             drain(scopy, 1, b)
             store(0, 2 * W, b, b + 1)
-        vector_piece(q0, bf0, a2, 2 * W, 2 * W, 0, E5M2)
+
+        piece(dy0_q, dy0_bf, dy0_last, 2 * W, 2 * W, 0, E5M2)
         for b in range(BLOCKS):
             opening(2, b)
         drain(scopy, 1, 0)
-        piece(q1, bf1, b2, 2 * W, 2 * W, SHARE, E5M2)
+        store(W, 2 * W, 0, 1)
+        piece(dy1_q, dy1_bf, dy1_last, 2 * W, 2 * W, LAST_SHARE, E5M2)
         drain(scopy, 1, 1)
-        store(W, 2 * W, 0, 2)
+        store(W, 2 * W, 1, 2)
         for b in range(BLOCKS):
             closing(2, b)
         for b in range(BLOCKS):

@@ -18,6 +18,7 @@ PACK = 4
 W = 512
 HALF = W // 2
 RUN = 4
+ALIGN = 256
 BLOCKS = R // P
 PASSES = K // W
 SHARE = 192
@@ -35,17 +36,17 @@ def tile_mix_lorab_none_kernel(tc, x, dn, hs_words, hs_scales, dy0, dy1, out):
         scopy = nc.scalar.copy
 
         def load(name, rows):
-            raw = sb.tile([P, PACK, rows.shape[1]], F32, name=name + "_raw")
+            raw = sb.tile([P, PACK, rows.shape[1]], F32, name=name + "_raw", align_bytes=ALIGN)
             nc.sync.dma_start(out=raw[:], in_=rows.rearrange("(p j) w -> p j w", j=PACK))
             return raw
 
         def operand(name, width):
-            codes = sb.tile([P, width], U32, name=name + "_codes", align_bytes=64)
-            scales = sb.tile([P, width], U8, name=name + "_scales", align_bytes=64)
+            codes = sb.tile([P, width], U32, name=name + "_codes", align_bytes=ALIGN)
+            scales = sb.tile([P, width], U8, name=name + "_scales", align_bytes=ALIGN)
             return codes, scales
 
         def staging(name, width):
-            return sb.tile([P, width * PACK], BF16, name=name + "_bf", align_bytes=64)
+            return sb.tile([P, width * PACK], BF16, name=name + "_bf", align_bytes=ALIGN)
 
         def cast(copy, bf, c0, c1, raw, first=0):
             copy(
@@ -132,7 +133,7 @@ def tile_mix_lorab_none_kernel(tc, x, dn, hs_words, hs_scales, dy0, dy1, out):
             )
 
         banks = {}
-        res = sb.tile([P, BLOCKS, N], F32, name="res")
+        res = sb.tile([P, BLOCKS, N], F32, name="res", align_bytes=ALIGN)
 
         def opening(k, b):
             banks[k, b] = ps.tile([P, W], F32, name="o_bank", tag="bank%d" % (b + BLOCKS * ((k + 1) % 2)))

@@ -188,9 +188,9 @@ def tile_mix_lorab_none_kernel(tc, x, dn, hs_words, hs_scales, dy0, dy1, out):
 
         for b in (2, 3, 0, 1):
             closing(1, b)
-        drain(scopy, 0, 0)
-        drain(scopy, 0, 1)
-        store(0, W, 0, 2)
+        for b in (0, 1):
+            drain(scopy, 0, b)
+            store(0, W, b, b + 1)
         drain(scopy, 0, 2)
         drain(scopy, 0, 3)
         for b in (2, 3):

from contextlib import ExitStack

import concourse.mybir as mybir

K, O, T, R, N = 1024, 512, 512, 512, 1536
FLOPS = 2 * K * T * R + 2 * (O + T) * R * N

F32 = mybir.dt.float32
BF16 = mybir.dt.bfloat16
U32 = mybir.dt.uint32
I32 = mybir.dt.int32
U8 = mybir.dt.uint8
E4M3 = mybir.dt.float8_e4m3fn_x4
E5M2 = mybir.dt.float8_e5m2_x4

P = 128
PACK = 4
W = 512
HALF = W // 2
RUN = 4
ALIGN = 256
BLOCKS = R // P
PASSES = K // W
SHARE = 192
LAST_SHARE = 160


def tile_mix_lorab_none_kernel(tc, x, dn, hs_words, hs_scales, dy0, dy1, out):
    nc = tc.nc
    with ExitStack() as ctx:
        sb = ctx.enter_context(tc.tile_pool(name="sb", bufs=1))
        ps = ctx.enter_context(tc.psum_pool(name="ps", bufs=1))
        ctx.enter_context(tc.manual_schedule())

        vcopy = nc.vector.tensor_copy
        scopy = nc.scalar.copy

        def load(name, rows):
            raw = sb.tile([P, PACK, rows.shape[1]], F32, name=name + "_raw", align_bytes=ALIGN)
            nc.sync.dma_start(out=raw[:], in_=rows.rearrange("(p j) w -> p j w", j=PACK))
            return raw

        def operand(name, width):
            codes = sb.tile([P, width], U32, name=name + "_codes", align_bytes=ALIGN)
            scales = sb.tile([P, width], U8, name=name + "_scales", align_bytes=ALIGN)
            return codes, scales

        def staging(name, width):
            return sb.tile([P, width * PACK], BF16, name=name + "_bf", align_bytes=ALIGN)

        def cast(copy, bf, c0, c1, raw, first=0):
            copy(
                out=bf[:, c0 * PACK : c1 * PACK].rearrange("p (c i j) -> p c j i", i=RUN, j=PACK),
                in_=raw[:, :, c0 - first : c1 - first].rearrange("p j (c i) -> p c j i", i=RUN),
            )

        def quantize(op, c0, c1, bf, fmt):
            nc.vector.quantize_mx(
                out=op[0][:, c0:c1].bitcast(fmt), scales=op[1][:, c0:c1], in_=bf[:, c0 * PACK : c1 * PACK]
            )

        def piece(op, bf, raw, c0, first, share, fmt):
            if share > 0:
                cast(scopy, bf, c0 + W - share, c0 + W, raw, first)
            cast(vcopy, bf, c0, c0 + HALF, raw, first)
            cast(vcopy, bf, c0 + HALF, c0 + W - share, raw, first)
            quantize(op, c0, c0 + HALF, bf, fmt)
            quantize(op, c0 + HALF, c0 + W, bf, fmt)

        def mx(acc, lhs, l0, lfmt, rhs, r0, rw, rfmt, start, stop):
            nc.tensor.matmul_mx(
                out=acc,
                lhsT=lhs[0][:, l0 : l0 + P].bitcast(lfmt),
                lhsT_scale=lhs[1][:, l0 : l0 + P],
                rhs=rhs[0][:, r0 : r0 + rw].bitcast(rfmt),
                rhs_scale=rhs[1][:, r0 : r0 + rw],
                start=start,
                stop=stop,
            )

        hs = operand("hs", R)
        nc.vector.memset(hs[1][:].bitcast(I32), 0)
        dy0_head = load("dy0_head", dy0[:, 0 : 2 * W])
        for q in range(4):
            nc.scalar.dma_start(
                out=hs[1][32 * q : 32 * q + 4, :].bitcast(I32),
                in_=hs_scales[0, 4 * q : 4 * q + 4, :].bitcast(I32),
            )
        x_raw = []
        dn_raw = []
        for g in range(PASSES):
            x_raw.append(load("x%d" % g, x[g * W : (g + 1) * W, :]))
            dn_raw.append(load("dn%d" % g, dn[g * W : (g + 1) * W, :]))
        nc.sync.dma_start(
            out=hs[0][:].bitcast(I32), in_=hs_words[0].rearrange("p r i -> p (r i)").bitcast(I32)
        )
        dy1_raw = [load("dy1_%d" % k, dy1[:, k * W : (k + 1) * W]) for k in range(2)]
        dy0_last = load("dy0_last", dy0[:, 2 * W :])
        dy1_last = load("dy1_last", dy1[:, 2 * W :])

        dy0_bf = staging("dy0", N)
        dy1_bf = staging("dy1", N)
        dy0_q = operand("dy0", N)
        dy1_q = operand("dy1", N)
        x_bf = [staging("x%d" % g, T) for g in range(PASSES)]
        x_q = [operand("x%d" % g, T) for g in range(PASSES)]
        dn_bf = [staging("dn%d" % g, R) for g in range(PASSES)]
        dn_q = [operand("dn%d" % g, R) for g in range(PASSES)]

        def quantize_x(g):
            x_out = x_bf[g][:].rearrange("p (i m j) -> p m j i", i=PACK, j=PACK)
            x_in = x_raw[g][:].rearrange("p j (m i) -> p m j i", i=PACK)
            cut = (T - SHARE) // PACK
            scopy(out=x_out[:, cut:], in_=x_in[:, cut:])
            vcopy(out=x_out[:, :cut], in_=x_in[:, :cut])
            quantize(x_q[g], 0, T, x_bf[g], E4M3)

        h_bank = [ps.tile([P, PACK, P], F32, name="h_bank", tag="bank%d" % b) for b in range(BLOCKS)]

        def h_pass(g, b):
            for i in range(PACK):
                opens = g == 0 and i == 0
                closes = g == PASSES - 1 and i == PACK - 1
                mx(h_bank[b][:, i, :], x_q[g], i * P, E4M3, dn_q[g], b * P, P, E4M3, opens, closes)

        h_bf = staging("h", R)
        h_q = operand("h", R)

        def h_out(copy, b):
            copy(
                out=h_bf[:, b * W : (b + 1) * W].rearrange("p (r i) -> p r i", i=PACK),
                in_=h_bank[b][:].rearrange("p i r -> p r i"),
            )

        banks = {}
        res = sb.tile([P, BLOCKS, N], F32, name="res", align_bytes=ALIGN)

        def opening(k, b):
            banks[k, b] = ps.tile([P, W], F32, name="o_bank", tag="bank%d" % (b + BLOCKS * ((k + 1) % 2)))
            mx(banks[k, b][:], hs, b * P, E4M3, dy0_q, k * W, W, E5M2, True, False)

        def closing(k, b):
            mx(banks[k, b][:], h_q, b * P, E4M3, dy1_q, k * W, W, E5M2, False, True)

        def drain(copy, k, b):
            copy(out=res[:, b, k * W : (k + 1) * W], in_=banks[k, b][:])

        def store(c0, c1, b0, b1):
            nc.sync.dma_start(
                out=out[b0 * P : b1 * P, c0:c1].rearrange("(b p) n -> p b n", p=P),
                in_=res[:, b0:b1, c0:c1],
            )

        for k in range(2):
            piece(dy0_q, dy0_bf, dy0_head, k * W, 0, SHARE, E5M2)
        quantize_x(0)
        piece(dn_q[0], dn_bf[0], dn_raw[0], 0, 0, SHARE, E4M3)
        for b in range(BLOCKS):
            h_pass(0, b)
        quantize_x(1)

        cast(scopy, dn_bf[1], 3 * P, 4 * P, dn_raw[1])
        cast(vcopy, dn_bf[1], 0, P, dn_raw[1])
        cast(vcopy, dn_bf[1], P, 2 * P, dn_raw[1])
        quantize(dn_q[1], 0, P, dn_bf[1], E4M3)
        cast(vcopy, dn_bf[1], 2 * P, 3 * P, dn_raw[1])
        for b in (1, 3, 2):
            quantize(dn_q[1], b * P, (b + 1) * P, dn_bf[1], E4M3)

        opening(0, 0)
        for b in range(BLOCKS):
            h_pass(1, b)
            h_out(vcopy if b == 1 else scopy, b)
        for b in range(1, BLOCKS):
            opening(0, b)
        for b in range(BLOCKS):
            opening(1, b)

        cast(vcopy, dy1_bf, 0, HALF, dy1_raw[0])
        cast(vcopy, dy1_bf, HALF, W, dy1_raw[0])
        quantize(h_q, 0, HALF, h_bf, E4M3)
        quantize(dy1_q, 0, HALF, dy1_bf, E5M2)
        quantize(dy1_q, HALF, W, dy1_bf, E5M2)
        quantize(h_q, HALF, R, h_bf, E4M3)
        for b in range(BLOCKS):
            closing(0, b)
        piece(dy1_q, dy1_bf, dy1_raw[1], W, W, 0, E5M2)

        for b in (2, 3, 0, 1):
            closing(1, b)
        for b in (0, 1):
            drain(scopy, 0, b)
            store(0, W, b, b + 1)
        drain(scopy, 0, 2)
        drain(scopy, 0, 3)
        for b in (2, 3):
            drain(scopy, 1, b)
            store(0, 2 * W, b, b + 1)

        piece(dy0_q, dy0_bf, dy0_last, 2 * W, 2 * W, 0, E5M2)
        for b in range(BLOCKS):
            opening(2, b)
        drain(scopy, 1, 0)
        store(W, 2 * W, 0, 1)
        piece(dy1_q, dy1_bf, dy1_last, 2 * W, 2 * W, LAST_SHARE, E5M2)
        drain(scopy, 1, 1)
        store(W, 2 * W, 1, 2)
        for b in range(BLOCKS):
            closing(2, b)
        for b in range(BLOCKS):
            drain(vcopy if b % 2 == 0 else scopy, 2, b)
            store(2 * W, N, b, b + 1)
